import numpy as np
import ml_dtypes


def mxq(x, axis, fmt="e4m3"):
    dtype, down = {"e4m3": (ml_dtypes.float8_e4m3fn, 7), "e5m2": (ml_dtypes.float8_e5m2, 14)}[fmt]
    v = np.moveaxis(np.asarray(x, np.float32).astype(ml_dtypes.bfloat16).astype(np.float64), axis, -1)
    blocks = v.reshape(v.shape[:-1] + (-1, 32))
    amax = np.abs(blocks).max(-1, keepdims=True)
    byte = np.maximum(np.where(amax > 0, np.frexp(amax)[1] - 1 + 127, 0) - down, 1)
    scale = np.exp2(byte - 127.0)
    codes = (blocks / scale).astype(np.float32).astype(dtype).astype(np.float64)
    return np.moveaxis((codes * scale).reshape(v.shape), -1, axis)


WIDE = False


def mx_kscale(k, group=512):
    if not WIDE:
        return np.ones(k)
    levels = np.array([10, -10, 5, -5, 0])
    if group != 512:
        return np.exp2(np.random.permutation(np.resize(levels, k // group))).repeat(group)
    if k % 512:
        return np.exp2(np.random.permutation(np.resize(levels, k // 32))).repeat(32)
    a = np.empty((k // 512, 16))
    for p in range(k // 512):
        a[p, :8] = np.random.permutation(np.resize(levels, 8))
        for g in range(8):
            far = levels[np.abs(levels - a[p, g]) >= 10]
            a[p, g + 8] = far[np.random.randint(len(far))]
    return np.exp2(a.ravel()).repeat(32)


def f64(x):
    return np.asarray(x).astype(np.float64)


G, D, M, O, N = 2, 256, 128, 256, 512


def setup_inputs():
    n = np.random.standard_normal
    s_d = mx_kscale(D, 0)
    s_o = mx_kscale(O, 0)
    return {
        "x": (n((G, D, N)) * s_d[:, None]).astype(np.float32),
        "w1": (n((G, D, M)) / np.sqrt(D) / s_d[:, None]).astype(np.float32),
        "w2": (n((G, D, M)) / np.sqrt(D) / s_d[:, None]).astype(np.float32),
        "fl": (np.random.uniform(0.05, 0.3, (G, M, 1))).astype(np.float32),
        "wo": (n((G, O, M)) / np.sqrt(O) / s_o[:, None]).astype(np.float32),
        "dy": (n((G, O, N)) * s_o[:, None]).astype(np.float32),
        "og": (np.random.uniform(0.3, 1.0, (G, M, 1))).astype(np.float32),
        "base": (0.2 * n((G, M, N))).astype(np.float32),
    }


def reference(x, w1, w2, fl, wo, dy, og, base):
    w1q = mxq(f64(w1), 1, "e4m3")
    xq = mxq(f64(x), 1, "e4m3")
    z1 = w1q.transpose(0, 2, 1) @ xq
    w2q = mxq(f64(w2), 1, "e4m3")
    z2 = w2q.transpose(0, 2, 1) @ xq
    e1 = np.exp(np.square(z1) * (-1.0))
    e2 = np.exp(np.square(z2) * (-1.0))
    woq = mxq(f64(wo), 1, "e4m3")
    dyq = mxq(f64(dy), 1, "e4m3")
    c0 = woq.transpose(0, 2, 1) @ dyq
    de1 = c0 * z2 / (e1 + e2 + f64(fl)) - c0 * z2 * e1 / np.square(e1 + e2 + f64(fl))
    dz1 = de1 * e1 * (-1.0) * z1 * 2.0
    kdz1 = dz1 * 2.0
    kde1 = kdz1 * 2.0 * z1 * (-1.0) * e1
    ke1 = kdz1 * 2.0 * z1 * (-1.0) * de1 + kde1 * (-1.0) / np.square(e1 + e2 + f64(fl)) * c0 * z2 + kde1 * (-1.0) * c0 * z2 * e1 / np.square(np.square(e1 + e2 + f64(fl))) * (-1.0) * (e1 + e2 + f64(fl)) * 2.0 - kde1 * c0 * z2 / np.square(e1 + e2 + f64(fl))
    kz1 = kdz1 * 2.0 * de1 * e1 * (-1.0) + ke1 * e1 * (-1.0) * z1 * 2.0
    y = kz1 * f64(og) + f64(base)
    return y

@@ -1,0 +1,296 @@
+from contextlib import ExitStack
+
+import concourse.mybir as mybir
+
+G, D, M, N = 2, 256, 128, 512
+FLOPS = 3 * 2 * G * D * M * N
+
+F32 = mybir.dt.float32
+BF16 = mybir.dt.bfloat16
+U32 = mybir.dt.uint32
+U8 = mybir.dt.uint8
+FP8X4 = mybir.dt.float8_e4m3fn_x4
+ALU = mybir.AluOpType
+ACT = mybir.ActivationFunctionType
+
+P = 128
+PACK = 4
+ROWS = D // PACK
+NT = 128
+HALF = N // 2
+X_CHUNKS = ((0, 128), (128, 128), (256, 128), (384, 128))
+SQUARE_CAP = 64.0
+
+
+def tile_rows_gpgaussshare_kernel(tc, x, w1, w2, fl, wo, dy, og, base, out):
+    nc = tc.nc
+
+    def packed_rows(t):
+        return t.rearrange("g (p j) c -> (g p) j c", j=PACK)
+
+    with ExitStack() as ctx:
+        sb = ctx.enter_context(tc.tile_pool(name="sb", bufs=1))
+        ps = ctx.enter_context(tc.psum_pool(name="ps", bufs=1))
+        ctx.enter_context(tc.manual_schedule())
+
+        def load(name, src, width):
+            raw = sb.tile([P, PACK, width], F32, name=name, align_bytes=64)
+            nc.sync.dma_start(out=raw[:], in_=src)
+            return raw
+
+        one = sb.tile([P, 1], F32, name="one")
+        nc.gpsimd.memset(one[:], 1.0)
+        floor = sb.tile([P, G], F32, name="floor")
+        gain = sb.tile([P, G], F32, name="gain")
+        with nc.allow_non_contiguous_dma(reason="one value a partition"):
+            nc.scalar.dma_start(out=floor[:], in_=fl.rearrange("g m o -> m (g o)"))
+            nc.scalar.dma_start(out=gain[:], in_=og.rearrange("g m o -> m (g o)"))
+
+        w1_raw = load("w1_raw", packed_rows(w1), M)
+        w2_raw = load("w2_raw", packed_rows(w2), M)
+        x_loads = [(c0, w, load("x_raw%d" % c0, packed_rows(x)[:, :, c0 : c0 + w], w)) for c0, w in ((0, 128), (128, 128), (256, 128), (384, 128))]
+        x_raw = [[r[:, :, k0 - c0 : k0 - c0 + kw] for c0, w, r in x_loads if c0 <= k0 < c0 + w][0] for k0, kw in X_CHUNKS]
+        wo_raw = load("wo_raw", packed_rows(wo), M)
+        dy_all = load("dy_all", packed_rows(dy), N)
+        dy_raw = [dy_all[:, :, h * HALF : (h + 1) * HALF] for h in range(2)]
+        base_sb = sb.tile([P, G, N], F32, name="base_sb")
+        nc.sync.dma_start(out=base_sb[:], in_=base.rearrange("g m n -> m g n"))
+
+        def operand(name, width):
+            words = sb.tile([P, width * PACK], BF16, name=name + "_bf", align_bytes=64)
+            codes = sb.tile([P, width], U32, name=name + "_codes", align_bytes=64)
+            scales = sb.tile([P, width], U8, name=name + "_scales", align_bytes=64)
+            return words, codes, scales
+
+        def interleave(copy, op, c0, raw):
+            width = raw.shape[2]
+            dst = op[0][:, c0 * PACK : (c0 + width) * PACK]
+            copy(
+                out=dst.rearrange("p (c i j) -> p c j i", i=4, j=PACK),
+                in_=raw[:].rearrange("p j (c i) -> p c j i", i=4),
+            )
+
+        def quantize(op):
+            nc.vector.quantize_mx(out=op[1][:].bitcast(FP8X4), scales=op[2][:], in_=op[0][:])
+
+        def product(dst, g, wop, w0, xop, x0):
+            rows = slice(g * ROWS, (g + 1) * ROWS)
+            nc.tensor.matmul_mx(
+                out=dst,
+                lhsT=wop[1][rows, w0 : w0 + M].bitcast(FP8X4),
+                lhsT_scale=wop[2][rows, w0 : w0 + M],
+                rhs=xop[1][rows, x0 : x0 + NT].bitcast(FP8X4),
+                rhs_scale=xop[2][rows, x0 : x0 + NT],
+                start=True,
+                stop=True,
+            )
+
+        w12 = operand("w12", 2 * M)
+        wo_op = operand("wo", M)
+        x_op = [operand("x%d" % k, w) for k, (c0, w) in enumerate(X_CHUNKS)]
+        dy_op = [operand("dy%d" % h, HALF) for h in range(2)]
+
+        z_ps = [[ps.tile([P, 2, w], F32, name="z%d_%d" % (k, g), tag="bank%d_%d" % (k, g)) for g in range(G)] for k, (c0, w) in enumerate(X_CHUNKS)]
+        c_ps = {}
+
+        sq = sb.tile([P, G, 2, N], F32, name="sq")
+        grow = sb.tile([P, G, N], F32, name="grow")
+        bell2 = sb.tile([P, G, N], F32, name="bell2")
+        odds = sb.tile([P, G, N], F32, name="odds")
+        lead = sb.tile([P, G, N], F32, name="lead")
+
+        def chunk_cols(k):
+            return slice(X_CHUNKS[k][0], X_CHUNKS[k][0] + X_CHUNKS[k][1])
+
+        def forward_products(k):
+            for g in range(G):
+                for i in range(2):
+                    for n0 in range(0, X_CHUNKS[k][1], NT):
+                        product(z_ps[k][g][:, i, n0 : n0 + NT], g, w12, i * M, x_op[k], n0)
+
+        def backward_products(h):
+            for g in range(G):
+                c_ps[h, g] = ps.tile([P, HALF], F32, name="c%d_%d" % (h, g), tag="bank%d_%d" % (1 - h, g))
+                for n0 in range(0, HALF, NT):
+                    product(c_ps[h, g][:, n0 : n0 + NT], g, wo_op, 0, dy_op[h], n0)
+
+        def squares(k):
+            for g in range(G):
+                nc.scalar.activation(out=sq[:, g, :, chunk_cols(k)], in_=z_ps[k][g][:], func=ACT.Square)
+
+        def cap(k):
+            a2 = sq[:, :, 0, chunk_cols(k)]
+            nc.vector.tensor_scalar(out=a2, in0=a2, scalar1=SQUARE_CAP, scalar2=None, op0=ALU.min)
+
+        def second_bell(k):
+            cols = chunk_cols(k)
+            nc.scalar.activation(out=bell2[:, :, cols], in_=sq[:, :, 1, cols], func=ACT.Exp, scale=-1.0)
+
+        def inverse_bell(k):
+            cols = chunk_cols(k)
+            nc.scalar.activation(out=grow[:, :, cols], in_=sq[:, :, 0, cols], func=ACT.Exp)
+
+        def weigh(h, g):
+            cols = slice(h * HALF, (h + 1) * HALF)
+            nc.vector.tensor_tensor(out=lead[:, g, cols], in0=c_ps[h, g][:], in1=lead[:, g, cols], op=ALU.mult)
+
+        def lead_factor(k, g):
+            cols = chunk_cols(k)
+            nc.vector.scalar_tensor_tensor(
+                out=lead[:, g, cols], in0=z_ps[k][g][:, 0, :], scalar=2.0, in1=sq[:, g, 1, cols], op0=ALU.mult, op1=ALU.mult
+            )
+
+        def make_odds(h, g):
+            cols = slice(h * HALF, (h + 1) * HALF)
+            nc.vector.scalar_tensor_tensor(
+                out=odds[:, g, cols], in0=bell2[:, g, cols], scalar=floor[:, g : g + 1], in1=grow[:, g, cols], op0=ALU.add, op1=ALU.mult
+            )
+
+        interleave(nc.scalar.copy, w12, 0, w1_raw)
+        interleave(nc.vector.tensor_copy, w12, M, w2_raw)
+        for i in range(2):
+            nc.vector.quantize_mx(out=w12[1][:, i * M : (i + 1) * M].bitcast(FP8X4), scales=w12[2][:, i * M : (i + 1) * M], in_=w12[0][:, i * M * PACK : (i + 1) * M * PACK])
+        interleave(nc.scalar.copy, x_op[0], 0, x_raw[0][:, :, 0:64])
+        interleave(nc.vector.tensor_copy, x_op[0], 64, x_raw[0][:, :, 64:128])
+        quantize(x_op[0])
+        forward_products(0)
+        interleave(nc.vector.tensor_copy, x_op[1], 0, x_raw[1])
+        quantize(x_op[1])
+        forward_products(1)
+        interleave(nc.vector.tensor_copy, x_op[2], 0, x_raw[2])
+        quantize(x_op[2])
+        forward_products(2)
+        squares(0)
+        cap(0)
+        second_bell(0)
+        lead_factor(0, 0)
+        lead_factor(0, 1)
+        interleave(nc.vector.tensor_copy, x_op[3], 0, x_raw[3])
+        squares(1)
+        inverse_bell(0)
+        interleave(nc.vector.tensor_copy, wo_op, 0, wo_raw)
+        quantize(x_op[3])
+        forward_products(3)
+        cap(1)
+        second_bell(1)
+        lead_factor(1, 0)
+        lead_factor(1, 1)
+        quantize(wo_op)
+        squares(2)
+        inverse_bell(1)
+        cap(2)
+        second_bell(2)
+        make_odds(0, 0)
+        make_odds(0, 1)
+        lead_factor(2, 0)
+        lead_factor(2, 1)
+        squares(3)
+        inverse_bell(2)
+        cap(3)
+        second_bell(3)
+        inverse_bell(3)
+        interleave(nc.vector.tensor_copy, dy_op[1], 0, dy_raw[1])
+        lead_factor(3, 0)
+        lead_factor(3, 1)
+        quantize(dy_op[1])
+        backward_products(1)
+        interleave(nc.vector.tensor_copy, dy_op[0], 0, dy_raw[0])
+        make_odds(1, 0)
+        quantize(dy_op[0])
+        backward_products(0)
+        make_odds(1, 1)
+
+        pieces = [(g, slice(h * HALF, (h + 1) * HALF)) for h in range(2) for g in range(G)]
+        count = len(pieces)
+        root = [sb.tile([P, HALF], F32, name="root%d" % i) for i in range(count)]
+        share = [sb.tile([P, HALF], F32, name="share%d" % i) for i in range(count)]
+        spread = [sb.tile([P, HALF], F32, name="spread%d" % i) for i in range(count)]
+        slope = [sb.tile([P, HALF], F32, name="slope%d" % i) for i in range(G)]
+        slope2 = [sb.tile([P, HALF], F32, name="slope2%d" % i) for i in range(count)]
+        bend = [sb.tile([P, HALF], F32, name="bend%d" % i) for i in range(count)]
+        factor = [sb.tile([P, HALF], F32, name="factor%d" % i) for i in range(count)]
+        grad = [sb.tile([P, HALF], F32, name="grad%d" % i) for i in range(count)]
+        result = [sb.tile([P, HALF], F32, name="result%d" % i) for i in range(count)]
+
+        def make_root(i):
+            g, cols = pieces[i]
+            nc.scalar.activation(out=root[i][:], in_=odds[:, g, cols], func=ACT.Abs_reciprocal_sqrt, bias=one[:])
+
+        def make_share(i):
+            nc.scalar.activation(out=share[i][:], in_=root[i][:], func=ACT.Square)
+
+        def make_spread(i):
+            nc.scalar.activation(out=spread[i][:], in_=share[i][:], func=ACT.Square, scale=-2.0, bias=one[:])
+
+        def make_bend(i):
+            g, cols = pieces[i]
+            nc.vector.scalar_tensor_tensor(
+                out=bend[i][:], in0=share[i][:], scalar=-0.5, in1=sq[:, g, 0, cols], op0=ALU.add, op1=ALU.mult
+            )
+
+        def make_slope(i):
+            g, cols = pieces[i]
+            nc.vector.scalar_tensor_tensor(
+                out=slope[i][:], in0=spread[i][:], scalar=-1.0, in1=c_ps[cols.start // HALF, g][:], op0=ALU.add, op1=ALU.mult
+            )
+
+        def make_slope2(i):
+            nc.scalar.activation(out=slope2[i][:], in_=slope[i][:], func=ACT.Square)
+
+        def make_factor(i):
+            g, cols = pieces[i]
+            nc.vector.scalar_tensor_tensor(
+                out=factor[i][:], in0=bend[i][:], scalar=0.25, in1=lead[:, g, cols], op0=ALU.add, op1=ALU.mult
+            )
+
+        def make_grad(i):
+            nc.vector.tensor_tensor(out=grad[i][:], in0=slope2[i][:], in1=factor[i][:], op=ALU.mult)
+
+        def finish(i):
+            g, cols = pieces[i]
+            nc.vector.scalar_tensor_tensor(
+                out=result[i][:], in0=grad[i][:], scalar=gain[:, g : g + 1], in1=base_sb[:, g, cols], op0=ALU.mult, op1=ALU.add
+            )
+            nc.sync.dma_start(out=out[g, :, cols], in_=result[i][:])
+
+        def make_width(i):
+            nc.scalar.activation(out=slope2[i][:], in_=spread[i][:], func=ACT.Square, scale=-1.0, bias=one[:])
+
+        make_root(0)
+        make_share(0)
+        make_root(1)
+        weigh(1, 0)
+        weigh(1, 1)
+        weigh(1, 0)
+        weigh(1, 1)
+        make_spread(0)
+        make_bend(0)
+        make_slope(0)
+        make_share(1)
+        make_factor(0)
+        make_root(2)
+        make_spread(1)
+        make_bend(1)
+        make_slope2(0)
+        make_slope(1)
+        make_root(3)
+        make_share(2)
+        make_slope2(1)
+        make_grad(0)
+        make_factor(1)
+        finish(0)
+        make_share(3)
+        make_spread(2)
+        make_bend(2)
+        make_grad(1)
+        make_spread(3)
+        make_bend(3)
+        finish(1)
+        make_width(2)
+        make_factor(2)
+        make_width(3)
+        make_factor(3)
+        make_grad(2)
+        make_grad(3)
+        finish(2)
+        finish(3)

@@ -40,21 +40,25 @@ def tile_rows_gpgaussshare_kernel(tc, x, w1, w2, fl, wo, dy, og, base, out):
 
         one = sb.tile([P, 1], F32, name="one")
         nc.gpsimd.memset(one[:], 1.0)
-        floor = sb.tile([P, G], F32, name="floor")
-        gain = sb.tile([P, G], F32, name="gain")
-        with nc.allow_non_contiguous_dma(reason="one value a partition"):
-            nc.scalar.dma_start(out=floor[:], in_=fl.rearrange("g m o -> m (g o)"))
-            nc.scalar.dma_start(out=gain[:], in_=og.rearrange("g m o -> m (g o)"))
+        def load_column(name, src):
+            col = sb.tile([P, G, 8], F32, name=name)
+            with nc.allow_non_contiguous_dma(reason="one value a partition and group"):
+                nc.sync.dma_start(out=col[:, :, 0:1], in_=src.rearrange("g m o -> m g o"))
+            return col
 
-        w1_raw = load("w1_raw", packed_rows(w1), M)
+        def load_x(k):
+            return load("x_raw%d" % k, packed_rows(x)[:, :, k * NT : (k + 1) * NT], NT)
+
         w2_raw = load("w2_raw", packed_rows(w2), M)
-        x_loads = [(c0, w, load("x_raw%d" % c0, packed_rows(x)[:, :, c0 : c0 + w], w)) for c0, w in ((0, 128), (128, 128), (256, 128), (384, 128))]
-        x_raw = [[r[:, :, k0 - c0 : k0 - c0 + kw] for c0, w, r in x_loads if c0 <= k0 < c0 + w][0] for k0, kw in X_CHUNKS]
+        x_raw = [load_x(0)]
+        w1_raw = load("w1_raw", packed_rows(w1), M)
+        x_raw.extend(load_x(k) for k in range(1, 4))
+        floor = load_column("floor", fl)
         wo_raw = load("wo_raw", packed_rows(wo), M)
-        dy_all = load("dy_all", packed_rows(dy), N)
-        dy_raw = [dy_all[:, :, h * HALF : (h + 1) * HALF] for h in range(2)]
+        dy_raw = {h: load("dy_raw%d" % h, packed_rows(dy)[:, :, h * HALF : (h + 1) * HALF], HALF) for h in (1, 0)}
         base_sb = sb.tile([P, G, N], F32, name="base_sb")
         nc.sync.dma_start(out=base_sb[:], in_=base.rearrange("g m n -> m g n"))
+        gain = load_column("gain", og)
 
         def operand(name, width):
             words = sb.tile([P, width * PACK], BF16, name=name + "_bf", align_bytes=64)
@@ -85,7 +89,7 @@ def tile_rows_gpgaussshare_kernel(tc, x, w1, w2, fl, wo, dy, og, base, out):
                 stop=True,
             )
 
-        w12 = operand("w12", 2 * M)
+        w_op = [operand("w1", M), operand("w2", M)]
         wo_op = operand("wo", M)
         x_op = [operand("x%d" % k, w) for k, (c0, w) in enumerate(X_CHUNKS)]
         dy_op = [operand("dy%d" % h, HALF) for h in range(2)]
@@ -102,11 +106,10 @@ def tile_rows_gpgaussshare_kernel(tc, x, w1, w2, fl, wo, dy, og, base, out):
         def chunk_cols(k):
             return slice(X_CHUNKS[k][0], X_CHUNKS[k][0] + X_CHUNKS[k][1])
 
-        def forward_products(k):
+        def forward_products(k, which=(0, 1)):
             for g in range(G):
-                for i in range(2):
-                    for n0 in range(0, X_CHUNKS[k][1], NT):
-                        product(z_ps[k][g][:, i, n0 : n0 + NT], g, w12, i * M, x_op[k], n0)
+                for i in which:
+                    product(z_ps[k][g][:, i, :], g, w_op[i], 0, x_op[k], 0)
 
         def backward_products(h):
             for g in range(G):
@@ -114,9 +117,9 @@ def tile_rows_gpgaussshare_kernel(tc, x, w1, w2, fl, wo, dy, og, base, out):
                 for n0 in range(0, HALF, NT):
                     product(c_ps[h, g][:, n0 : n0 + NT], g, wo_op, 0, dy_op[h], n0)
 
-        def squares(k):
+        def squares(k, which=slice(0, 2)):
             for g in range(G):
-                nc.scalar.activation(out=sq[:, g, :, chunk_cols(k)], in_=z_ps[k][g][:], func=ACT.Square)
+                nc.scalar.activation(out=sq[:, g, which, chunk_cols(k)], in_=z_ps[k][g][:, which, :], func=ACT.Square)
 
         def cap(k):
             a2 = sq[:, :, 0, chunk_cols(k)]
@@ -143,36 +146,38 @@ def tile_rows_gpgaussshare_kernel(tc, x, w1, w2, fl, wo, dy, og, base, out):
         def make_odds(h, g):
             cols = slice(h * HALF, (h + 1) * HALF)
             nc.vector.scalar_tensor_tensor(
-                out=odds[:, g, cols], in0=bell2[:, g, cols], scalar=floor[:, g : g + 1], in1=grow[:, g, cols], op0=ALU.add, op1=ALU.mult
+                out=odds[:, g, cols], in0=bell2[:, g, cols], scalar=floor[:, g, 0:1], in1=grow[:, g, cols], op0=ALU.add, op1=ALU.mult
             )
 
-        interleave(nc.scalar.copy, w12, 0, w1_raw)
-        interleave(nc.vector.tensor_copy, w12, M, w2_raw)
-        for i in range(2):
-            nc.vector.quantize_mx(out=w12[1][:, i * M : (i + 1) * M].bitcast(FP8X4), scales=w12[2][:, i * M : (i + 1) * M], in_=w12[0][:, i * M * PACK : (i + 1) * M * PACK])
-        interleave(nc.scalar.copy, x_op[0], 0, x_raw[0][:, :, 0:64])
-        interleave(nc.vector.tensor_copy, x_op[0], 64, x_raw[0][:, :, 64:128])
+        interleave(nc.vector.tensor_copy, w_op[1], 0, w2_raw)
+        quantize(w_op[1])
+        interleave(nc.scalar.copy, x_op[0], 0, x_raw[0][:, :, 0:48])
+        interleave(nc.vector.tensor_copy, x_op[0], 48, x_raw[0][:, :, 48:128])
         quantize(x_op[0])
-        forward_products(0)
+        forward_products(0, (1,))
+        interleave(nc.vector.tensor_copy, w_op[0], 0, w1_raw)
+        squares(0, slice(1, 2))
+        quantize(w_op[0])
+        forward_products(0, (0,))
         interleave(nc.vector.tensor_copy, x_op[1], 0, x_raw[1])
         quantize(x_op[1])
         forward_products(1)
+        second_bell(0)
+        squares(0, slice(0, 1))
         interleave(nc.vector.tensor_copy, x_op[2], 0, x_raw[2])
+        cap(0)
         quantize(x_op[2])
         forward_products(2)
-        squares(0)
-        cap(0)
-        second_bell(0)
         lead_factor(0, 0)
         lead_factor(0, 1)
         interleave(nc.vector.tensor_copy, x_op[3], 0, x_raw[3])
         squares(1)
         inverse_bell(0)
-        interleave(nc.vector.tensor_copy, wo_op, 0, wo_raw)
+        cap(1)
         quantize(x_op[3])
         forward_products(3)
-        cap(1)
         second_bell(1)
+        interleave(nc.vector.tensor_copy, wo_op, 0, wo_raw)
         lead_factor(1, 0)
         lead_factor(1, 1)
         quantize(wo_op)
@@ -180,24 +185,24 @@ def tile_rows_gpgaussshare_kernel(tc, x, w1, w2, fl, wo, dy, og, base, out):
         inverse_bell(1)
         cap(2)
         second_bell(2)
+        interleave(nc.vector.tensor_copy, dy_op[1], 0, dy_raw[1])
         make_odds(0, 0)
-        make_odds(0, 1)
-        lead_factor(2, 0)
-        lead_factor(2, 1)
         squares(3)
         inverse_bell(2)
         cap(3)
         second_bell(3)
         inverse_bell(3)
-        interleave(nc.vector.tensor_copy, dy_op[1], 0, dy_raw[1])
-        lead_factor(3, 0)
-        lead_factor(3, 1)
         quantize(dy_op[1])
         backward_products(1)
+        make_odds(0, 1)
+        lead_factor(2, 0)
+        lead_factor(2, 1)
         interleave(nc.vector.tensor_copy, dy_op[0], 0, dy_raw[0])
-        make_odds(1, 0)
+        lead_factor(3, 0)
+        lead_factor(3, 1)
         quantize(dy_op[0])
         backward_products(0)
+        make_odds(1, 0)
         make_odds(1, 1)
 
         pieces = [(g, slice(h * HALF, (h + 1) * HALF)) for h in range(2) for g in range(G)]
@@ -249,7 +254,7 @@ def tile_rows_gpgaussshare_kernel(tc, x, w1, w2, fl, wo, dy, og, base, out):
         def finish(i):
             g, cols = pieces[i]
             nc.vector.scalar_tensor_tensor(
-                out=result[i][:], in0=grad[i][:], scalar=gain[:, g : g + 1], in1=base_sb[:, g, cols], op0=ALU.mult, op1=ALU.add
+                out=result[i][:], in0=grad[i][:], scalar=gain[:, g, 0:1], in1=base_sb[:, g, cols], op0=ALU.mult, op1=ALU.add
             )
             nc.sync.dma_start(out=out[g, :, cols], in_=result[i][:])
 

from contextlib import ExitStack

import concourse.mybir as mybir

G, D, M, N = 2, 256, 128, 512
FLOPS = 3 * 2 * G * D * M * N

F32 = mybir.dt.float32
BF16 = mybir.dt.bfloat16
U32 = mybir.dt.uint32
U8 = mybir.dt.uint8
FP8X4 = mybir.dt.float8_e4m3fn_x4
ALU = mybir.AluOpType
ACT = mybir.ActivationFunctionType

P = 128
PACK = 4
ROWS = D // PACK
NT = 128
HALF = N // 2
X_CHUNKS = ((0, 128), (128, 128), (256, 128), (384, 128))
SQUARE_CAP = 64.0


def tile_rows_gpgaussshare_kernel(tc, x, w1, w2, fl, wo, dy, og, base, out):
    nc = tc.nc

    def packed_rows(t):
        return t.rearrange("g (p j) c -> (g p) j c", j=PACK)

    with ExitStack() as ctx:
        sb = ctx.enter_context(tc.tile_pool(name="sb", bufs=1))
        ps = ctx.enter_context(tc.psum_pool(name="ps", bufs=1))
        ctx.enter_context(tc.manual_schedule())

        def load(name, src, width):
            raw = sb.tile([P, PACK, width], F32, name=name, align_bytes=64)
            nc.sync.dma_start(out=raw[:], in_=src)
            return raw

        one = sb.tile([P, 1], F32, name="one")
        nc.gpsimd.memset(one[:], 1.0)
        def load_column(name, src):
            col = sb.tile([P, G, 8], F32, name=name)
            with nc.allow_non_contiguous_dma(reason="one value a partition and group"):
                nc.sync.dma_start(out=col[:, :, 0:1], in_=src.rearrange("g m o -> m g o"))
            return col

        def load_x(k):
            return load("x_raw%d" % k, packed_rows(x)[:, :, k * NT : (k + 1) * NT], NT)

        w2_raw = load("w2_raw", packed_rows(w2), M)
        x_raw = [load_x(0)]
        w1_raw = load("w1_raw", packed_rows(w1), M)
        x_raw.extend(load_x(k) for k in range(1, 4))
        floor = load_column("floor", fl)
        wo_raw = load("wo_raw", packed_rows(wo), M)
        dy_raw = {h: load("dy_raw%d" % h, packed_rows(dy)[:, :, h * HALF : (h + 1) * HALF], HALF) for h in (1, 0)}
        base_sb = sb.tile([P, G, N], F32, name="base_sb")
        nc.sync.dma_start(out=base_sb[:], in_=base.rearrange("g m n -> m g n"))
        gain = load_column("gain", og)

        def operand(name, width):
            words = sb.tile([P, width * PACK], BF16, name=name + "_bf", align_bytes=64)
            codes = sb.tile([P, width], U32, name=name + "_codes", align_bytes=64)
            scales = sb.tile([P, width], U8, name=name + "_scales", align_bytes=64)
            return words, codes, scales

        def interleave(copy, op, c0, raw):
            width = raw.shape[2]
            dst = op[0][:, c0 * PACK : (c0 + width) * PACK]
            copy(
                out=dst.rearrange("p (c i j) -> p c j i", i=4, j=PACK),
                in_=raw[:].rearrange("p j (c i) -> p c j i", i=4),
            )

        def quantize(op):
            nc.vector.quantize_mx(out=op[1][:].bitcast(FP8X4), scales=op[2][:], in_=op[0][:])

        def product(dst, g, wop, w0, xop, x0):
            rows = slice(g * ROWS, (g + 1) * ROWS)
            nc.tensor.matmul_mx(
                out=dst,
                lhsT=wop[1][rows, w0 : w0 + M].bitcast(FP8X4),
                lhsT_scale=wop[2][rows, w0 : w0 + M],
                rhs=xop[1][rows, x0 : x0 + NT].bitcast(FP8X4),
                rhs_scale=xop[2][rows, x0 : x0 + NT],
                start=True,
                stop=True,
            )

        w_op = [operand("w1", M), operand("w2", M)]
        wo_op = operand("wo", M)
        x_op = [operand("x%d" % k, w) for k, (c0, w) in enumerate(X_CHUNKS)]
        dy_op = [operand("dy%d" % h, HALF) for h in range(2)]

        z_ps = [[ps.tile([P, 2, w], F32, name="z%d_%d" % (k, g), tag="bank%d_%d" % (k, g)) for g in range(G)] for k, (c0, w) in enumerate(X_CHUNKS)]
        c_ps = {}

        sq = sb.tile([P, G, 2, N], F32, name="sq")
        grow = sb.tile([P, G, N], F32, name="grow")
        bell2 = sb.tile([P, G, N], F32, name="bell2")
        odds = sb.tile([P, G, N], F32, name="odds")
        lead = sb.tile([P, G, N], F32, name="lead")

        def chunk_cols(k):
            return slice(X_CHUNKS[k][0], X_CHUNKS[k][0] + X_CHUNKS[k][1])

        def forward_products(k, which=(0, 1)):
            for g in range(G):
                for i in which:
                    product(z_ps[k][g][:, i, :], g, w_op[i], 0, x_op[k], 0)

        def backward_products(h):
            for g in range(G):
                c_ps[h, g] = ps.tile([P, HALF], F32, name="c%d_%d" % (h, g), tag="bank%d_%d" % (1 - h, g))
                for n0 in range(0, HALF, NT):
                    product(c_ps[h, g][:, n0 : n0 + NT], g, wo_op, 0, dy_op[h], n0)

        def squares(k, which=slice(0, 2)):
            for g in range(G):
                nc.scalar.activation(out=sq[:, g, which, chunk_cols(k)], in_=z_ps[k][g][:, which, :], func=ACT.Square)

        def cap(k):
            a2 = sq[:, :, 0, chunk_cols(k)]
            nc.vector.tensor_scalar(out=a2, in0=a2, scalar1=SQUARE_CAP, scalar2=None, op0=ALU.min)

        def second_bell(k):
            cols = chunk_cols(k)
            nc.scalar.activation(out=bell2[:, :, cols], in_=sq[:, :, 1, cols], func=ACT.Exp, scale=-1.0)

        def inverse_bell(k):
            cols = chunk_cols(k)
            nc.scalar.activation(out=grow[:, :, cols], in_=sq[:, :, 0, cols], func=ACT.Exp)

        def weigh(h, g):
            cols = slice(h * HALF, (h + 1) * HALF)
            nc.vector.tensor_tensor(out=lead[:, g, cols], in0=c_ps[h, g][:], in1=lead[:, g, cols], op=ALU.mult)

        def lead_factor(k, g):
            cols = chunk_cols(k)
            nc.vector.scalar_tensor_tensor(
                out=lead[:, g, cols], in0=z_ps[k][g][:, 0, :], scalar=2.0, in1=sq[:, g, 1, cols], op0=ALU.mult, op1=ALU.mult
            )

        def make_odds(h, g):
            cols = slice(h * HALF, (h + 1) * HALF)
            nc.vector.scalar_tensor_tensor(
                out=odds[:, g, cols], in0=bell2[:, g, cols], scalar=floor[:, g, 0:1], in1=grow[:, g, cols], op0=ALU.add, op1=ALU.mult
            )

        interleave(nc.vector.tensor_copy, w_op[1], 0, w2_raw)
        quantize(w_op[1])
        interleave(nc.scalar.copy, x_op[0], 0, x_raw[0][:, :, 0:48])
        interleave(nc.vector.tensor_copy, x_op[0], 48, x_raw[0][:, :, 48:128])
        quantize(x_op[0])
        forward_products(0, (1,))
        interleave(nc.vector.tensor_copy, w_op[0], 0, w1_raw)
        squares(0, slice(1, 2))
        quantize(w_op[0])
        forward_products(0, (0,))
        interleave(nc.vector.tensor_copy, x_op[1], 0, x_raw[1])
        quantize(x_op[1])
        forward_products(1)
        second_bell(0)
        squares(0, slice(0, 1))
        interleave(nc.vector.tensor_copy, x_op[2], 0, x_raw[2])
        cap(0)
        quantize(x_op[2])
        forward_products(2)
        lead_factor(0, 0)
        lead_factor(0, 1)
        interleave(nc.vector.tensor_copy, x_op[3], 0, x_raw[3])
        squares(1)
        inverse_bell(0)
        cap(1)
        quantize(x_op[3])
        forward_products(3)
        second_bell(1)
        interleave(nc.vector.tensor_copy, wo_op, 0, wo_raw)
        lead_factor(1, 0)
        lead_factor(1, 1)
        quantize(wo_op)
        squares(2)
        inverse_bell(1)
        cap(2)
        second_bell(2)
        interleave(nc.vector.tensor_copy, dy_op[1], 0, dy_raw[1])
        make_odds(0, 0)
        squares(3)
        inverse_bell(2)
        cap(3)
        second_bell(3)
        inverse_bell(3)
        quantize(dy_op[1])
        backward_products(1)
        make_odds(0, 1)
        lead_factor(2, 0)
        lead_factor(2, 1)
        interleave(nc.vector.tensor_copy, dy_op[0], 0, dy_raw[0])
        lead_factor(3, 0)
        lead_factor(3, 1)
        quantize(dy_op[0])
        backward_products(0)
        make_odds(1, 0)
        make_odds(1, 1)

        pieces = [(g, slice(h * HALF, (h + 1) * HALF)) for h in range(2) for g in range(G)]
        count = len(pieces)
        root = [sb.tile([P, HALF], F32, name="root%d" % i) for i in range(count)]
        share = [sb.tile([P, HALF], F32, name="share%d" % i) for i in range(count)]
        spread = [sb.tile([P, HALF], F32, name="spread%d" % i) for i in range(count)]
        slope = [sb.tile([P, HALF], F32, name="slope%d" % i) for i in range(G)]
        slope2 = [sb.tile([P, HALF], F32, name="slope2%d" % i) for i in range(count)]
        bend = [sb.tile([P, HALF], F32, name="bend%d" % i) for i in range(count)]
        factor = [sb.tile([P, HALF], F32, name="factor%d" % i) for i in range(count)]
        grad = [sb.tile([P, HALF], F32, name="grad%d" % i) for i in range(count)]
        result = [sb.tile([P, HALF], F32, name="result%d" % i) for i in range(count)]

        def make_root(i):
            g, cols = pieces[i]
            nc.scalar.activation(out=root[i][:], in_=odds[:, g, cols], func=ACT.Abs_reciprocal_sqrt, bias=one[:])

        def make_share(i):
            nc.scalar.activation(out=share[i][:], in_=root[i][:], func=ACT.Square)

        def make_spread(i):
            nc.scalar.activation(out=spread[i][:], in_=share[i][:], func=ACT.Square, scale=-2.0, bias=one[:])

        def make_bend(i):
            g, cols = pieces[i]
            nc.vector.scalar_tensor_tensor(
                out=bend[i][:], in0=share[i][:], scalar=-0.5, in1=sq[:, g, 0, cols], op0=ALU.add, op1=ALU.mult
            )

        def make_slope(i):
            g, cols = pieces[i]
            nc.vector.scalar_tensor_tensor(
                out=slope[i][:], in0=spread[i][:], scalar=-1.0, in1=c_ps[cols.start // HALF, g][:], op0=ALU.add, op1=ALU.mult
            )

        def make_slope2(i):
            nc.scalar.activation(out=slope2[i][:], in_=slope[i][:], func=ACT.Square)

        def make_factor(i):
            g, cols = pieces[i]
            nc.vector.scalar_tensor_tensor(
                out=factor[i][:], in0=bend[i][:], scalar=0.25, in1=lead[:, g, cols], op0=ALU.add, op1=ALU.mult
            )

        def make_grad(i):
            nc.vector.tensor_tensor(out=grad[i][:], in0=slope2[i][:], in1=factor[i][:], op=ALU.mult)

        def finish(i):
            g, cols = pieces[i]
            nc.vector.scalar_tensor_tensor(
                out=result[i][:], in0=grad[i][:], scalar=gain[:, g, 0:1], in1=base_sb[:, g, cols], op0=ALU.mult, op1=ALU.add
            )
            nc.sync.dma_start(out=out[g, :, cols], in_=result[i][:])

        def make_width(i):
            nc.scalar.activation(out=slope2[i][:], in_=spread[i][:], func=ACT.Square, scale=-1.0, bias=one[:])

        make_root(0)
        make_share(0)
        make_root(1)
        weigh(1, 0)
        weigh(1, 1)
        weigh(1, 0)
        weigh(1, 1)
        make_spread(0)
        make_bend(0)
        make_slope(0)
        make_share(1)
        make_factor(0)
        make_root(2)
        make_spread(1)
        make_bend(1)
        make_slope2(0)
        make_slope(1)
        make_root(3)
        make_share(2)
        make_slope2(1)
        make_grad(0)
        make_factor(1)
        finish(0)
        make_share(3)
        make_spread(2)
        make_bend(2)
        make_grad(1)
        make_spread(3)
        make_bend(3)
        finish(1)
        make_width(2)
        make_factor(2)
        make_width(3)
        make_factor(3)
        make_grad(2)
        make_grad(3)
        finish(2)
        finish(3)
